import numpy as np
import ml_dtypes


def mxq(x, axis, fmt="e4m3"):
    dtype, down = {"e4m3": (ml_dtypes.float8_e4m3fn, 7), "e5m2": (ml_dtypes.float8_e5m2, 14)}[fmt]
    v = np.moveaxis(np.asarray(x, np.float32).astype(ml_dtypes.bfloat16).astype(np.float64), axis, -1)
    blocks = v.reshape(v.shape[:-1] + (-1, 32))
    amax = np.abs(blocks).max(-1, keepdims=True)
    byte = np.maximum(np.where(amax > 0, np.frexp(amax)[1] - 1 + 127, 0) - down, 1)
    scale = np.exp2(byte - 127.0)
    codes = (blocks / scale).astype(np.float32).astype(dtype).astype(np.float64)
    return np.moveaxis((codes * scale).reshape(v.shape), -1, axis)


WIDE = False


def mx_kscale(k):
    if not WIDE:
        return np.ones(k)
    levels = np.array([10, -10, 5, -5, 0])
    if k % 512:
        return np.exp2(np.random.permutation(np.resize(levels, k // 32))).repeat(32)
    a = np.empty((k // 512, 16))
    for p in range(k // 512):
        a[p, :8] = np.random.permutation(np.resize(levels, 8))
        for g in range(8):
            far = levels[np.abs(levels - a[p, g]) >= 10]
            a[p, g + 8] = far[np.random.randint(len(far))]
    return np.exp2(a.ravel()).repeat(32)


def f64(x):
    return np.asarray(x).astype(np.float64)


def striped(idx):
    return np.tile(np.asarray(idx).reshape(-1, 16).T, (8, 1)).astype(np.uint16)


def unstriped(offs):
    return offs[:16].T.reshape(-1).astype(np.int64)


E2M1 = np.array([0.0, 0.5, 1.0, 1.5, 2.0, 3.0, 4.0, 6.0, -0.0, -0.5, -1.0, -1.5, -2.0, -3.0, -4.0, -6.0])


def pack_weight(w, fmt):
    k, n = w.shape
    w = f64(np.asarray(w, np.float32).astype(ml_dtypes.bfloat16)).reshape(k // 32, 32, n)
    amax = np.abs(w).max(1)
    if fmt == "e4m3":
        byte = np.frexp(amax)[1] - 1 + 127 - 7
    else:
        mant, ex = np.frexp(amax / 6.0)
        byte = np.where(mant > 0.5, ex, ex - 1) + 127
    byte = np.clip(np.where(amax > 0, byte, 1), 1, 254)
    scaled = (w * np.exp2(127.0 - byte)[:, None, :]).reshape(k, n).astype(np.float32)
    by_word = np.ascontiguousarray(scaled.reshape(k // 512, 128, 4, n).transpose(0, 1, 3, 2))
    if fmt == "e4m3":
        words = by_word.astype(ml_dtypes.float8_e4m3fn).view(np.uint8)
    else:
        c = by_word.astype(ml_dtypes.float4_e2m1fn).view(np.uint8) & 0xF
        words = (c[..., 0::2] | (c[..., 1::2] << 4)).reshape(k // 512, 128, 2 * n)
    return np.ascontiguousarray(words), np.ascontiguousarray(byte.astype(np.uint8).reshape(k // 512, 16, n))


def unpack_weight(words, scales, fmt):
    g, _, n = scales.shape
    words = np.ascontiguousarray(words).reshape(g, 128, n, -1)
    if fmt == "e4m3":
        vals = words.view(ml_dtypes.float8_e4m3fn).astype(np.float64)
    else:
        nib = np.empty((g, 128, n, 4), np.uint8)
        nib[..., 0::2] = words & 0xF
        nib[..., 1::2] = words >> 4
        vals = E2M1[nib]
    vals = vals * np.repeat(np.exp2(scales.astype(np.float64) - 127.0), 8, axis=1)[..., None]
    return vals.transpose(0, 1, 3, 2).reshape(g * 512, n)


def sigmoid(v):
    return 1.0 / (1.0 + np.exp(-v))


def bf(x):
    return np.asarray(x, np.float32).astype(ml_dtypes.bfloat16)


def planes(Y):
    r, m = Y.shape
    b = f64(bf(Y)).reshape(r // 32, 32, m)
    amax = np.abs(b).max(1)
    byte = np.clip(np.where(amax > 0, np.frexp(amax)[1] - 1 + 127 - 7, 1), 1, 254)
    codes = (b * np.exp2(127.0 - byte)[:, None, :]).reshape(r, m).astype(np.float32).astype(ml_dtypes.float8_e4m3fn).view(np.uint8)
    words = codes.reshape(r // 512, 128, 4, m).transpose(0, 1, 3, 2)
    return np.ascontiguousarray(words), np.ascontiguousarray(byte.astype(np.uint8).reshape(r // 512, 16, m))


K, T, J, L, N = 512, 2048, 512, 512, 512


def setup_inputs():
    n = np.random.standard_normal
    idx = np.random.permutation(T)[:J]
    fk = mx_kscale(K)
    fl = mx_kscale(L)
    wp = pack_weight(n((K, N)) * 1 / np.sqrt(K) * fk[:, None], "e4m3")
    pxp = pack_weight(n((L, J)) / fl[:, None], "e2m1")
    wpp = pack_weight(n((L, N)) * 1 / np.sqrt(L) * fl[:, None], "e4m3")
    return {
        "xf": (n((K, T)) / fk[:, None]).astype(np.float32),
        "w_words": wp[0],
        "w_scales": wp[1],
        "px_words": pxp[0],
        "px_scales": pxp[1],
        "wp_words": wpp[0],
        "wp_scales": wpp[1],
        "offs": striped(idx),
    }


def reference(xf, w_words, w_scales, px_words, px_scales, wp_words, wp_scales, offs):
    idx = unstriped(offs)
    wu = unpack_weight(w_words, w_scales, "e4m3")
    pxu = unpack_weight(px_words, px_scales, "e2m1")
    wpu = unpack_weight(wp_words, wp_scales, "e4m3")
    xg = f64(xf)[:, idx]
    xp = np.pad(xg, ((0, 0), (1, 0)))[:, :J]
    d = xg - xp
    dq = mxq(d, 0, "e4m3")
    p = wu.T @ dq
    q = wpu.T @ pxu
    y = p * sigmoid(q)
    words, scales = planes(y)
    return y, words, scales

@@ -1,0 +1,189 @@
+from contextlib import ExitStack
+
+import concourse.mybir as mybir
+
+K, T, J, L, N = 512, 2048, 512, 512, 512
+FLOPS = 2 * K * N * J + 2 * L * N * J
+
+F32 = mybir.dt.float32
+BF16 = mybir.dt.bfloat16
+I32 = mybir.dt.int32
+U16 = mybir.dt.uint16
+U8 = mybir.dt.uint8
+FP8X4 = mybir.dt.float8_e4m3fn_x4
+FP4X4 = mybir.dt.float4_e2m1fn_x4
+SUB = mybir.AluOpType.subtract
+MULT = mybir.AluOpType.mult
+SIGMOID = mybir.ActivationFunctionType.Sigmoid
+
+P = 128
+PACK = 4
+PAD = 8
+CH = 128
+NCH = J // CH
+W_ROW = 4
+
+
+def tile_list_steps_along_track_pl_kernel(
+    tc, xf, w_words, w_scales, px_words, px_scales, wp_words, wp_scales, offs, out_0, out_1, out_2
+):
+    nc = tc.nc
+    with ExitStack() as ctx:
+        sb = ctx.enter_context(tc.tile_pool(name="sb", bufs=1))
+        ps = ctx.enter_context(tc.psum_pool(name="ps", bufs=1))
+
+        offsets = sb.tile([P, J // 16], U16, name="offsets")
+        x_planes = [sb.tile([P, T], F32, name=f"x{t}") for t in range(PACK)]
+        w_raw = sb.tile([P, N], I32, name="w_raw")
+        wp_raw = sb.tile([P, N], I32, name="wp_raw")
+        px_codes = sb.tile([P, 2 * J], U8, name="px_codes", align_bytes=64)
+        ws_raw = sb.tile([P, N], U8, name="ws_raw", align_bytes=64)
+        px_plane = sb.tile([P, J], U8, name="px_plane", align_bytes=64)
+
+        xf_planes = xf.rearrange("(p t) c -> p t c", t=PACK)
+        nc.vector.memset(ws_raw[:].bitcast(I32), 0)
+        nc.vector.memset(px_plane[:].bitcast(I32), 0)
+
+        nc.sync.dma_start(offsets[:], offs)
+        nc.sync.dma_start(x_planes[0][:], xf_planes[:, 0, :])
+        nc.sync.dma_start(wp_raw[:], wp_words[0].rearrange("p n t -> p (n t)").bitcast(I32))
+        nc.sync.dma_start(w_raw[:], w_words[0].rearrange("p n t -> p (n t)").bitcast(I32))
+        nc.sync.dma_start(px_codes[:].bitcast(I32), px_words[0].bitcast(I32))
+        for t in range(1, PACK):
+            nc.sync.dma_start(x_planes[t][:], xf_planes[:, t, :])
+        for scales, plane, row in ((wp_scales, ws_raw, 0), (w_scales, ws_raw, W_ROW), (px_scales, px_plane, 0)):
+            for q in range(4):
+                nc.scalar.dma_start(
+                    plane[32 * q + row : 32 * q + row + 4, :].bitcast(I32),
+                    scales[0, 4 * q : 4 * q + 4, :].bitcast(I32),
+                )
+
+        picked = [sb.tile([P, PAD + J], F32, name=f"picked{t}") for t in range(PACK)]
+        steps = [sb.tile([P, 2, J], BF16, name=f"steps{u}") for u in range(2)]
+        woven = sb.tile([P, J, PACK], BF16, name="woven", align_bytes=64)
+        for t in range(PACK):
+            nc.vector.memset(picked[t][:, 0:PAD], 0.0)
+
+        def gather(t, j0, j1):
+            nc.vector.tensor_copy(
+                picked[t][:, PAD + j0 : PAD + j1],
+                x_planes[t][:].indirect(offsets[:, j0 // 16 : j1 // 16]),
+            )
+
+        def subtract(t, j0, j1):
+            nc.vector.tensor_tensor(
+                steps[t // 2][:, t % 2, j0:j1],
+                picked[t][:, PAD + j0 : PAD + j1],
+                picked[t][:, PAD + j0 - 1 : PAD + j1 - 1],
+                SUB,
+            )
+
+        def weave(u, j0, j1):
+            nc.scalar.copy(
+                woven[:, j0:j1, 2 * u : 2 * u + 2],
+                steps[u][:, :, j0:j1].rearrange("p e j -> p j e"),
+            )
+
+        gather(0, 0, J)
+        subtract(0, 0, J)
+
+        w_dealt = sb.tile([P, PACK, P], I32, name="w_dealt", align_bytes=64)
+        wp_dealt = sb.tile([P, PACK, P], I32, name="wp_dealt", align_bytes=64)
+        ws_dealt = sb.tile([P, PACK, P], U8, name="ws_dealt", align_bytes=64)
+        for raw, dealt in ((wp_raw, wp_dealt), (w_raw, w_dealt), (ws_raw, ws_dealt)):
+            nc.vector.tensor_copy(
+                dealt[:].rearrange("p t m -> p m t"), raw[:].rearrange("p (m t) -> p m t", t=PACK)
+            )
+
+        gate = sb.tile([P, NCH, PACK, CH], F32, name="gate")
+        for t in range(PACK):
+            q_bank = ps.tile([P, J], F32, name=f"q_bank{t}")
+            nc.tensor.matmul_mx(
+                out=q_bank[:],
+                lhsT=wp_dealt[:, t, :].bitcast(FP8X4),
+                lhsT_scale=ws_dealt[:, t, :],
+                rhs=px_codes[:].bitcast(FP4X4),
+                rhs_scale=px_plane[:],
+                start=True,
+                stop=True,
+            )
+            nc.scalar.activation(gate[:, :, t, :], q_bank[:].rearrange("p (c j) -> p c j", j=CH), SIGMOID)
+
+        gather(1, 0, J)
+        subtract(1, 0, J)
+        weave(0, 0, J)
+        gather(2, 0, J)
+        subtract(2, 0, J)
+
+        d_codes = sb.tile([P, J], I32, name="d_codes", align_bytes=64)
+        d_plane = sb.tile([P, J], U8, name="d_plane", align_bytes=64)
+        y_codes = sb.tile([P, J], I32, name="y_codes", align_bytes=64)
+        y_plane = sb.tile([P, J], U8, name="y_plane", align_bytes=64)
+        y_rows = out_0.rearrange("(p t) j -> p t j", t=PACK)
+        words_out = out_1[0].rearrange("p j t -> p (j t)").bitcast(I32)
+        p_banks = [ps.tile([P, PACK, CH], F32, name=f"p_bank{c}") for c in range(NCH)]
+        ys = [sb.tile([P, PACK, CH], F32, name=f"y{c}") for c in range(NCH)]
+        y_wovens = [sb.tile([P, CH, PACK], BF16, name=f"y_woven{c}", align_bytes=64) for c in range(NCH)]
+
+        def cols(c):
+            return slice(c * CH, (c + 1) * CH)
+
+        def product(c):
+            nc.vector.quantize_mx(
+                out=d_codes[:, cols(c)].bitcast(FP8X4),
+                scales=d_plane[:, cols(c)],
+                in_=woven[:, cols(c), :].rearrange("p j t -> p (j t)"),
+            )
+            for t in range(PACK):
+                nc.tensor.matmul_mx(
+                    out=p_banks[c][:, t, :],
+                    lhsT=w_dealt[:, t, :].bitcast(FP8X4),
+                    lhsT_scale=ws_dealt[W_ROW:P, t, :],
+                    rhs=d_codes[:, cols(c)].bitcast(FP8X4),
+                    rhs_scale=d_plane[:, cols(c)],
+                    start=True,
+                    stop=True,
+                )
+
+        def gated(c):
+            nc.vector.tensor_tensor(ys[c][:], p_banks[c][:], gate[:, c, :, :], MULT)
+            nc.sync.dma_start(y_rows[:, :, cols(c)], ys[c][:])
+            nc.scalar.copy(
+                y_wovens[c][:].rearrange("p (g i) t -> p g t i", i=4),
+                ys[c][:].rearrange("p t (g i) -> p g t i", i=4),
+            )
+
+        def planes(c):
+            nc.vector.quantize_mx(
+                out=y_codes[:, cols(c)].bitcast(FP8X4),
+                scales=y_plane[:, cols(c)],
+                in_=y_wovens[c][:].rearrange("p j t -> p (j t)"),
+            )
+            if c % 2 == 1:
+                half = slice((c - 1) * CH, (c + 1) * CH)
+                nc.sync.dma_start(words_out[:, half], y_codes[:, half])
+
+        last = PACK - 1
+        for h in range(2):
+            gather(last, 2 * h * CH, 2 * (h + 1) * CH)
+            for c in (2 * h, 2 * h + 1):
+                subtract(last, c * CH, (c + 1) * CH)
+                weave(1, c * CH, (c + 1) * CH)
+        product(0)
+        product(1)
+        gated(0)
+        product(2)
+        product(3)
+        gated(1)
+        planes(0)
+        gated(2)
+        planes(1)
+        gated(3)
+        planes(2)
+        planes(3)
+        for q in range(4):
+            eng = nc.sync if q % 2 == 0 else nc.scalar
+            eng.dma_start(
+                out_2[0, 4 * q : 4 * q + 4, :].bitcast(I32),
+                y_plane[32 * q : 32 * q + 4, :].bitcast(I32),
+            )

@@ -42,21 +42,39 @@ def tile_list_steps_along_track_pl_kernel(
 
         xf_planes = xf.rearrange("(p t) c -> p t c", t=PACK)
         nc.vector.memset(ws_raw[:].bitcast(I32), 0)
-        nc.vector.memset(px_plane[:].bitcast(I32), 0)
+        nc.gpsimd.memset(px_plane[:].bitcast(I32), 0)
+        warm = sb.tile([P, 16], F32, name="warm")
+        nc.vector.memset(warm[:, 0:1], 0.0)
+        nc.scalar.activation(warm[:, 8:9], warm[:, 0:1], SIGMOID)
 
+        def load_scale_rows(queue, scales, plane, row, q):
+            queue.dma_start(
+                plane[32 * q + row : 32 * q + row + 4, :].bitcast(I32),
+                scales[0, 4 * q : 4 * q + 4, :].bitcast(I32),
+            )
+
+        def load_plane(t):
+            nc.sync.dma_start(x_planes[t][:], xf_planes[:, t, :])
+
+        scale_loads = [
+            (nc.sync, scales, ws_raw, row, q)
+            for scales, row in ((wp_scales, 0), (w_scales, W_ROW))
+            for q in range(4)
+        ]
+        for q in range(4):
+            load_scale_rows(nc.gpsimd, px_scales, px_plane, 0, q)
         nc.sync.dma_start(offsets[:], offs)
-        nc.sync.dma_start(x_planes[0][:], xf_planes[:, 0, :])
         nc.sync.dma_start(wp_raw[:], wp_words[0].rearrange("p n t -> p (n t)").bitcast(I32))
         nc.sync.dma_start(w_raw[:], w_words[0].rearrange("p n t -> p (n t)").bitcast(I32))
         nc.sync.dma_start(px_codes[:].bitcast(I32), px_words[0].bitcast(I32))
-        for t in range(1, PACK):
-            nc.sync.dma_start(x_planes[t][:], xf_planes[:, t, :])
-        for scales, plane, row in ((wp_scales, ws_raw, 0), (w_scales, ws_raw, W_ROW), (px_scales, px_plane, 0)):
-            for q in range(4):
-                nc.scalar.dma_start(
-                    plane[32 * q + row : 32 * q + row + 4, :].bitcast(I32),
-                    scales[0, 4 * q : 4 * q + 4, :].bitcast(I32),
-                )
+        for args in scale_loads[0:3]:
+            load_scale_rows(*args)
+        load_plane(0)
+        for args in scale_loads[3:8]:
+            load_scale_rows(*args)
+        load_plane(1)
+        load_plane(2)
+        load_plane(3)
 
         picked = [sb.tile([P, PAD + J], F32, name=f"picked{t}") for t in range(PACK)]
         steps = [sb.tile([P, 2, J], BF16, name=f"steps{u}") for u in range(2)]
@@ -84,16 +102,20 @@ def tile_list_steps_along_track_pl_kernel(
                 steps[u][:, :, j0:j1].rearrange("p e j -> p j e"),
             )
 
-        gather(0, 0, J)
-        subtract(0, 0, J)
-
         w_dealt = sb.tile([P, PACK, P], I32, name="w_dealt", align_bytes=64)
         wp_dealt = sb.tile([P, PACK, P], I32, name="wp_dealt", align_bytes=64)
         ws_dealt = sb.tile([P, PACK, P], U8, name="ws_dealt", align_bytes=64)
-        for raw, dealt in ((wp_raw, wp_dealt), (w_raw, w_dealt), (ws_raw, ws_dealt)):
+
+        def deal(raw, dealt):
             nc.vector.tensor_copy(
                 dealt[:].rearrange("p t m -> p m t"), raw[:].rearrange("p (m t) -> p m t", t=PACK)
             )
+
+        deal(wp_raw, wp_dealt)
+        deal(w_raw, w_dealt)
+        deal(ws_raw, ws_dealt)
+        gather(0, 0, J)
+        subtract(0, 0, J)
 
         gate = sb.tile([P, NCH, PACK, CH], F32, name="gate")
         for t in range(PACK):
@@ -148,7 +170,7 @@ def tile_list_steps_along_track_pl_kernel(
         def gated(c):
             nc.vector.tensor_tensor(ys[c][:], p_banks[c][:], gate[:, c, :, :], MULT)
             nc.sync.dma_start(y_rows[:, :, cols(c)], ys[c][:])
-            nc.scalar.copy(
+            (nc.vector.tensor_copy if c == NCH - 1 else nc.scalar.copy)(
                 y_wovens[c][:].rearrange("p (g i) t -> p g t i", i=4),
                 ys[c][:].rearrange("p t (g i) -> p g t i", i=4),
             )

@@ -21,7 +21,6 @@ PACK = 4
 PAD = 8
 CH = 128
 NCH = J // CH
-W_ROW = 4
 
 
 def tile_list_steps_along_track_pl_kernel(
@@ -38,43 +37,38 @@ def tile_list_steps_along_track_pl_kernel(
         wp_raw = sb.tile([P, N], I32, name="wp_raw")
         px_codes = sb.tile([P, 2 * J], U8, name="px_codes", align_bytes=64)
         ws_raw = sb.tile([P, N], U8, name="ws_raw", align_bytes=64)
+        wps_raw = sb.tile([P, N], U8, name="wps_raw", align_bytes=64)
         px_plane = sb.tile([P, J], U8, name="px_plane", align_bytes=64)
 
         xf_planes = xf.rearrange("(p t) c -> p t c", t=PACK)
-        nc.vector.memset(ws_raw[:].bitcast(I32), 0)
+        nc.vector.memset(wps_raw[:].bitcast(I32), 0)
         nc.gpsimd.memset(px_plane[:].bitcast(I32), 0)
+        nc.gpsimd.memset(ws_raw[:].bitcast(I32), 0)
         warm = sb.tile([P, 16], F32, name="warm")
         nc.vector.memset(warm[:, 0:1], 0.0)
         nc.scalar.activation(warm[:, 8:9], warm[:, 0:1], SIGMOID)
 
-        def load_scale_rows(queue, scales, plane, row, q):
-            queue.dma_start(
-                plane[32 * q + row : 32 * q + row + 4, :].bitcast(I32),
-                scales[0, 4 * q : 4 * q + 4, :].bitcast(I32),
-            )
+        def load_scale_rows(scales, plane):
+            for q in range(4):
+                nc.sync.dma_start(
+                    plane[32 * q : 32 * q + 4, :].bitcast(I32),
+                    scales[0, 4 * q : 4 * q + 4, :].bitcast(I32),
+                )
 
         def load_plane(t):
             nc.sync.dma_start(x_planes[t][:], xf_planes[:, t, :])
 
-        scale_loads = [
-            (nc.sync, scales, ws_raw, row, q)
-            for scales, row in ((wp_scales, 0), (w_scales, W_ROW))
-            for q in range(4)
-        ]
-        for q in range(4):
-            load_scale_rows(nc.gpsimd, px_scales, px_plane, 0, q)
-        nc.sync.dma_start(offsets[:], offs)
         nc.sync.dma_start(wp_raw[:], wp_words[0].rearrange("p n t -> p (n t)").bitcast(I32))
-        nc.sync.dma_start(w_raw[:], w_words[0].rearrange("p n t -> p (n t)").bitcast(I32))
         nc.sync.dma_start(px_codes[:].bitcast(I32), px_words[0].bitcast(I32))
-        for args in scale_loads[0:3]:
-            load_scale_rows(*args)
+        nc.sync.dma_start(offsets[:], offs)
+        load_scale_rows(wp_scales, wps_raw)
         load_plane(0)
-        for args in scale_loads[3:8]:
-            load_scale_rows(*args)
+        load_scale_rows(px_scales, px_plane)
         load_plane(1)
+        load_scale_rows(w_scales, ws_raw)
         load_plane(2)
         load_plane(3)
+        nc.sync.dma_start(w_raw[:], w_words[0].rearrange("p n t -> p (n t)").bitcast(I32))
 
         picked = [sb.tile([P, PAD + J], F32, name=f"picked{t}") for t in range(PACK)]
         steps = [sb.tile([P, 2, J], BF16, name=f"steps{u}") for u in range(2)]
@@ -96,8 +90,8 @@ def tile_list_steps_along_track_pl_kernel(
                 SUB,
             )
 
-        def weave(u, j0, j1):
-            nc.scalar.copy(
+        def weave(copy, u, j0, j1):
+            copy(
                 woven[:, j0:j1, 2 * u : 2 * u + 2],
                 steps[u][:, :, j0:j1].rearrange("p e j -> p j e"),
             )
@@ -105,6 +99,7 @@ def tile_list_steps_along_track_pl_kernel(
         w_dealt = sb.tile([P, PACK, P], I32, name="w_dealt", align_bytes=64)
         wp_dealt = sb.tile([P, PACK, P], I32, name="wp_dealt", align_bytes=64)
         ws_dealt = sb.tile([P, PACK, P], U8, name="ws_dealt", align_bytes=64)
+        wps_dealt = sb.tile([P, PACK, P], U8, name="wps_dealt", align_bytes=64)
 
         def deal(raw, dealt):
             nc.vector.tensor_copy(
@@ -112,8 +107,7 @@ def tile_list_steps_along_track_pl_kernel(
             )
 
         deal(wp_raw, wp_dealt)
-        deal(w_raw, w_dealt)
-        deal(ws_raw, ws_dealt)
+        deal(wps_raw, wps_dealt)
         gather(0, 0, J)
         subtract(0, 0, J)
 
@@ -123,7 +117,7 @@ def tile_list_steps_along_track_pl_kernel(
             nc.tensor.matmul_mx(
                 out=q_bank[:],
                 lhsT=wp_dealt[:, t, :].bitcast(FP8X4),
-                lhsT_scale=ws_dealt[:, t, :],
+                lhsT_scale=wps_dealt[:, t, :],
                 rhs=px_codes[:].bitcast(FP4X4),
                 rhs_scale=px_plane[:],
                 start=True,
@@ -133,7 +127,8 @@ def tile_list_steps_along_track_pl_kernel(
 
         gather(1, 0, J)
         subtract(1, 0, J)
-        weave(0, 0, J)
+        weave(nc.scalar.copy, 0, 0, J)
+        deal(ws_raw, ws_dealt)
         gather(2, 0, J)
         subtract(2, 0, J)
 
@@ -145,22 +140,25 @@ def tile_list_steps_along_track_pl_kernel(
         words_out = out_1[0].rearrange("p j t -> p (j t)").bitcast(I32)
         p_banks = [ps.tile([P, PACK, CH], F32, name=f"p_bank{c}") for c in range(NCH)]
         ys = [sb.tile([P, PACK, CH], F32, name=f"y{c}") for c in range(NCH)]
-        y_wovens = [sb.tile([P, CH, PACK], BF16, name=f"y_woven{c}", align_bytes=64) for c in range(NCH)]
+        y_woven = sb.tile([P, J, PACK], BF16, name="y_woven", align_bytes=64)
 
         def cols(c):
             return slice(c * CH, (c + 1) * CH)
 
-        def product(c):
+        def quantise_steps(c0, c1):
+            run = slice(c0 * CH, c1 * CH)
             nc.vector.quantize_mx(
-                out=d_codes[:, cols(c)].bitcast(FP8X4),
-                scales=d_plane[:, cols(c)],
-                in_=woven[:, cols(c), :].rearrange("p j t -> p (j t)"),
+                out=d_codes[:, run].bitcast(FP8X4),
+                scales=d_plane[:, run],
+                in_=woven[:, run, :].rearrange("p j t -> p (j t)"),
             )
+
+        def product(c):
             for t in range(PACK):
                 nc.tensor.matmul_mx(
                     out=p_banks[c][:, t, :],
                     lhsT=w_dealt[:, t, :].bitcast(FP8X4),
-                    lhsT_scale=ws_dealt[W_ROW:P, t, :],
+                    lhsT_scale=ws_dealt[:, t, :],
                     rhs=d_codes[:, cols(c)].bitcast(FP8X4),
                     rhs_scale=d_plane[:, cols(c)],
                     start=True,
@@ -171,38 +169,52 @@ def tile_list_steps_along_track_pl_kernel(
             nc.vector.tensor_tensor(ys[c][:], p_banks[c][:], gate[:, c, :, :], MULT)
             nc.sync.dma_start(y_rows[:, :, cols(c)], ys[c][:])
             (nc.vector.tensor_copy if c == NCH - 1 else nc.scalar.copy)(
-                y_wovens[c][:].rearrange("p (g i) t -> p g t i", i=4),
+                y_woven[:, cols(c), :].rearrange("p (g i) t -> p g t i", i=4),
                 ys[c][:].rearrange("p t (g i) -> p g t i", i=4),
             )
 
-        def planes(c):
+        def planes(c0, c1):
+            run = slice(c0 * CH, c1 * CH)
             nc.vector.quantize_mx(
-                out=y_codes[:, cols(c)].bitcast(FP8X4),
-                scales=y_plane[:, cols(c)],
-                in_=y_wovens[c][:].rearrange("p j t -> p (j t)"),
+                out=y_codes[:, run].bitcast(FP8X4),
+                scales=y_plane[:, run],
+                in_=y_woven[:, run, :].rearrange("p j t -> p (j t)"),
             )
-            if c % 2 == 1:
-                half = slice((c - 1) * CH, (c + 1) * CH)
-                nc.sync.dma_start(words_out[:, half], y_codes[:, half])
+
+        def store_words(c0, c1):
+            run = slice(c0 * CH, c1 * CH)
+            nc.sync.dma_start(words_out[:, run], y_codes[:, run])
 
         last = PACK - 1
-        for h in range(2):
-            gather(last, 2 * h * CH, 2 * (h + 1) * CH)
-            for c in (2 * h, 2 * h + 1):
-                subtract(last, c * CH, (c + 1) * CH)
-                weave(1, c * CH, (c + 1) * CH)
+        gather(last, 0, 256)
+        gather(last, 256, 512)
+        subtract(last, 0, 256)
+        weave(nc.scalar.copy, 1, 0, 128)
+        weave(nc.scalar.copy, 1, 128, 256)
+        subtract(last, 256, 512)
+        deal(w_raw, w_dealt)
+        quantise_steps(0, 1)
         product(0)
+        weave(nc.vector.tensor_copy, 1, 256, 512)
+        quantise_steps(1, 2)
         product(1)
-        gated(0)
+        quantise_steps(2, 4)
         product(2)
         product(3)
+        gated(0)
         gated(1)
-        planes(0)
         gated(2)
-        planes(1)
-        gated(3)
-        planes(2)
-        planes(3)
+        nc.vector.tensor_tensor(ys[3][:], p_banks[3][:], gate[:, 3, :, :], MULT)
+        nc.sync.dma_start(y_rows[:, :, cols(3)], ys[3][:])
+        planes(0, 2)
+        store_words(0, 2)
+        nc.vector.tensor_copy(
+            y_woven[:, cols(3), :].rearrange("p (g i) t -> p g t i", i=4),
+            ys[3][:].rearrange("p t (g i) -> p g t i", i=4),
+        )
+        planes(2, 3)
+        planes(3, 4)
+        store_words(2, 4)
         for q in range(4):
             eng = nc.sync if q % 2 == 0 else nc.scalar
             eng.dma_start(

from contextlib import ExitStack

import concourse.mybir as mybir

K, T, J, L, N = 512, 2048, 512, 512, 512
FLOPS = 2 * K * N * J + 2 * L * N * J

F32 = mybir.dt.float32
BF16 = mybir.dt.bfloat16
I32 = mybir.dt.int32
U16 = mybir.dt.uint16
U8 = mybir.dt.uint8
FP8X4 = mybir.dt.float8_e4m3fn_x4
FP4X4 = mybir.dt.float4_e2m1fn_x4
SUB = mybir.AluOpType.subtract
MULT = mybir.AluOpType.mult
SIGMOID = mybir.ActivationFunctionType.Sigmoid

P = 128
PACK = 4
PAD = 8
CH = 128
NCH = J // CH


def tile_list_steps_along_track_pl_kernel(
    tc, xf, w_words, w_scales, px_words, px_scales, wp_words, wp_scales, offs, out_0, out_1, out_2
):
    nc = tc.nc
    with ExitStack() as ctx:
        sb = ctx.enter_context(tc.tile_pool(name="sb", bufs=1))
        ps = ctx.enter_context(tc.psum_pool(name="ps", bufs=1))

        offsets = sb.tile([P, J // 16], U16, name="offsets")
        x_planes = [sb.tile([P, T], F32, name=f"x{t}") for t in range(PACK)]
        w_raw = sb.tile([P, N], I32, name="w_raw")
        wp_raw = sb.tile([P, N], I32, name="wp_raw")
        px_codes = sb.tile([P, 2 * J], U8, name="px_codes", align_bytes=64)
        ws_raw = sb.tile([P, N], U8, name="ws_raw", align_bytes=64)
        wps_raw = sb.tile([P, N], U8, name="wps_raw", align_bytes=64)
        px_plane = sb.tile([P, J], U8, name="px_plane", align_bytes=64)

        xf_planes = xf.rearrange("(p t) c -> p t c", t=PACK)
        nc.vector.memset(wps_raw[:].bitcast(I32), 0)
        nc.gpsimd.memset(px_plane[:].bitcast(I32), 0)
        nc.gpsimd.memset(ws_raw[:].bitcast(I32), 0)
        warm = sb.tile([P, 16], F32, name="warm")
        nc.vector.memset(warm[:, 0:1], 0.0)
        nc.scalar.activation(warm[:, 8:9], warm[:, 0:1], SIGMOID)

        def load_scale_rows(scales, plane):
            for q in range(4):
                nc.sync.dma_start(
                    plane[32 * q : 32 * q + 4, :].bitcast(I32),
                    scales[0, 4 * q : 4 * q + 4, :].bitcast(I32),
                )

        def load_plane(t):
            nc.sync.dma_start(x_planes[t][:], xf_planes[:, t, :])

        nc.sync.dma_start(wp_raw[:], wp_words[0].rearrange("p n t -> p (n t)").bitcast(I32))
        nc.sync.dma_start(px_codes[:].bitcast(I32), px_words[0].bitcast(I32))
        nc.sync.dma_start(offsets[:], offs)
        load_scale_rows(wp_scales, wps_raw)
        load_plane(0)
        load_scale_rows(px_scales, px_plane)
        load_plane(1)
        load_scale_rows(w_scales, ws_raw)
        load_plane(2)
        load_plane(3)
        nc.sync.dma_start(w_raw[:], w_words[0].rearrange("p n t -> p (n t)").bitcast(I32))

        picked = [sb.tile([P, PAD + J], F32, name=f"picked{t}") for t in range(PACK)]
        steps = [sb.tile([P, 2, J], BF16, name=f"steps{u}") for u in range(2)]
        woven = sb.tile([P, J, PACK], BF16, name="woven", align_bytes=64)
        for t in range(PACK):
            nc.vector.memset(picked[t][:, 0:PAD], 0.0)

        def gather(t, j0, j1):
            nc.vector.tensor_copy(
                picked[t][:, PAD + j0 : PAD + j1],
                x_planes[t][:].indirect(offsets[:, j0 // 16 : j1 // 16]),
            )

        def subtract(t, j0, j1):
            nc.vector.tensor_tensor(
                steps[t // 2][:, t % 2, j0:j1],
                picked[t][:, PAD + j0 : PAD + j1],
                picked[t][:, PAD + j0 - 1 : PAD + j1 - 1],
                SUB,
            )

        def weave(copy, u, j0, j1):
            copy(
                woven[:, j0:j1, 2 * u : 2 * u + 2],
                steps[u][:, :, j0:j1].rearrange("p e j -> p j e"),
            )

        w_dealt = sb.tile([P, PACK, P], I32, name="w_dealt", align_bytes=64)
        wp_dealt = sb.tile([P, PACK, P], I32, name="wp_dealt", align_bytes=64)
        ws_dealt = sb.tile([P, PACK, P], U8, name="ws_dealt", align_bytes=64)
        wps_dealt = sb.tile([P, PACK, P], U8, name="wps_dealt", align_bytes=64)

        def deal(raw, dealt):
            nc.vector.tensor_copy(
                dealt[:].rearrange("p t m -> p m t"), raw[:].rearrange("p (m t) -> p m t", t=PACK)
            )

        deal(wp_raw, wp_dealt)
        deal(wps_raw, wps_dealt)
        gather(0, 0, J)
        subtract(0, 0, J)

        gate = sb.tile([P, NCH, PACK, CH], F32, name="gate")
        for t in range(PACK):
            q_bank = ps.tile([P, J], F32, name=f"q_bank{t}")
            nc.tensor.matmul_mx(
                out=q_bank[:],
                lhsT=wp_dealt[:, t, :].bitcast(FP8X4),
                lhsT_scale=wps_dealt[:, t, :],
                rhs=px_codes[:].bitcast(FP4X4),
                rhs_scale=px_plane[:],
                start=True,
                stop=True,
            )
            nc.scalar.activation(gate[:, :, t, :], q_bank[:].rearrange("p (c j) -> p c j", j=CH), SIGMOID)

        gather(1, 0, J)
        subtract(1, 0, J)
        weave(nc.scalar.copy, 0, 0, J)
        deal(ws_raw, ws_dealt)
        gather(2, 0, J)
        subtract(2, 0, J)

        d_codes = sb.tile([P, J], I32, name="d_codes", align_bytes=64)
        d_plane = sb.tile([P, J], U8, name="d_plane", align_bytes=64)
        y_codes = sb.tile([P, J], I32, name="y_codes", align_bytes=64)
        y_plane = sb.tile([P, J], U8, name="y_plane", align_bytes=64)
        y_rows = out_0.rearrange("(p t) j -> p t j", t=PACK)
        words_out = out_1[0].rearrange("p j t -> p (j t)").bitcast(I32)
        p_banks = [ps.tile([P, PACK, CH], F32, name=f"p_bank{c}") for c in range(NCH)]
        ys = [sb.tile([P, PACK, CH], F32, name=f"y{c}") for c in range(NCH)]
        y_woven = sb.tile([P, J, PACK], BF16, name="y_woven", align_bytes=64)

        def cols(c):
            return slice(c * CH, (c + 1) * CH)

        def quantise_steps(c0, c1):
            run = slice(c0 * CH, c1 * CH)
            nc.vector.quantize_mx(
                out=d_codes[:, run].bitcast(FP8X4),
                scales=d_plane[:, run],
                in_=woven[:, run, :].rearrange("p j t -> p (j t)"),
            )

        def product(c):
            for t in range(PACK):
                nc.tensor.matmul_mx(
                    out=p_banks[c][:, t, :],
                    lhsT=w_dealt[:, t, :].bitcast(FP8X4),
                    lhsT_scale=ws_dealt[:, t, :],
                    rhs=d_codes[:, cols(c)].bitcast(FP8X4),
                    rhs_scale=d_plane[:, cols(c)],
                    start=True,
                    stop=True,
                )

        def gated(c):
            nc.vector.tensor_tensor(ys[c][:], p_banks[c][:], gate[:, c, :, :], MULT)
            nc.sync.dma_start(y_rows[:, :, cols(c)], ys[c][:])
            (nc.vector.tensor_copy if c == NCH - 1 else nc.scalar.copy)(
                y_woven[:, cols(c), :].rearrange("p (g i) t -> p g t i", i=4),
                ys[c][:].rearrange("p t (g i) -> p g t i", i=4),
            )

        def planes(c0, c1):
            run = slice(c0 * CH, c1 * CH)
            nc.vector.quantize_mx(
                out=y_codes[:, run].bitcast(FP8X4),
                scales=y_plane[:, run],
                in_=y_woven[:, run, :].rearrange("p j t -> p (j t)"),
            )

        def store_words(c0, c1):
            run = slice(c0 * CH, c1 * CH)
            nc.sync.dma_start(words_out[:, run], y_codes[:, run])

        last = PACK - 1
        gather(last, 0, 256)
        gather(last, 256, 512)
        subtract(last, 0, 256)
        weave(nc.scalar.copy, 1, 0, 128)
        weave(nc.scalar.copy, 1, 128, 256)
        subtract(last, 256, 512)
        deal(w_raw, w_dealt)
        quantise_steps(0, 1)
        product(0)
        weave(nc.vector.tensor_copy, 1, 256, 512)
        quantise_steps(1, 2)
        product(1)
        quantise_steps(2, 4)
        product(2)
        product(3)
        gated(0)
        gated(1)
        gated(2)
        nc.vector.tensor_tensor(ys[3][:], p_banks[3][:], gate[:, 3, :, :], MULT)
        nc.sync.dma_start(y_rows[:, :, cols(3)], ys[3][:])
        planes(0, 2)
        store_words(0, 2)
        nc.vector.tensor_copy(
            y_woven[:, cols(3), :].rearrange("p (g i) t -> p g t i", i=4),
            ys[3][:].rearrange("p t (g i) -> p g t i", i=4),
        )
        planes(2, 3)
        planes(3, 4)
        store_words(2, 4)
        for q in range(4):
            eng = nc.sync if q % 2 == 0 else nc.scalar
            eng.dma_start(
                out_2[0, 4 * q : 4 * q + 4, :].bitcast(I32),
                y_plane[32 * q : 32 * q + 4, :].bitcast(I32),
            )
